import numpy as np
import ml_dtypes


def mxq(x, axis, fmt="e4m3"):
    dtype, down = {"e4m3": (ml_dtypes.float8_e4m3fn, 7), "e5m2": (ml_dtypes.float8_e5m2, 14)}[fmt]
    v = np.moveaxis(np.asarray(x, np.float32).astype(ml_dtypes.bfloat16).astype(np.float64), axis, -1)
    blocks = v.reshape(v.shape[:-1] + (-1, 32))
    amax = np.abs(blocks).max(-1, keepdims=True)
    byte = np.maximum(np.where(amax > 0, np.frexp(amax)[1] - 1 + 127, 0) - down, 1)
    scale = np.exp2(byte - 127.0)
    codes = (blocks / scale).astype(np.float32).astype(dtype).astype(np.float64)
    return np.moveaxis((codes * scale).reshape(v.shape), -1, axis)


WIDE = False


def mx_kscale(k):
    if not WIDE:
        return np.ones(k)
    levels = np.array([10, -10, 5, -5, 0])
    if k % 512:
        return np.exp2(np.random.permutation(np.resize(levels, k // 32))).repeat(32)
    a = np.empty((k // 512, 16))
    for p in range(k // 512):
        a[p, :8] = np.random.permutation(np.resize(levels, 8))
        for g in range(8):
            far = levels[np.abs(levels - a[p, g]) >= 10]
            a[p, g + 8] = far[np.random.randint(len(far))]
    return np.exp2(a.ravel()).repeat(32)


def f64(x):
    return np.asarray(x).astype(np.float64)


def striped(idx):
    return np.tile(np.asarray(idx).reshape(-1, 16).T, (8, 1)).astype(np.uint16)


def unstriped(offs):
    return offs[:16].T.reshape(-1).astype(np.int64)


E2M1 = np.array([0.0, 0.5, 1.0, 1.5, 2.0, 3.0, 4.0, 6.0, -0.0, -0.5, -1.0, -1.5, -2.0, -3.0, -4.0, -6.0])


def pack_weight(w, fmt):
    k, n = w.shape
    w = f64(np.asarray(w, np.float32).astype(ml_dtypes.bfloat16)).reshape(k // 32, 32, n)
    amax = np.abs(w).max(1)
    if fmt == "e4m3":
        byte = np.frexp(amax)[1] - 1 + 127 - 7
    else:
        mant, ex = np.frexp(amax / 6.0)
        byte = np.where(mant > 0.5, ex, ex - 1) + 127
    byte = np.clip(np.where(amax > 0, byte, 1), 1, 254)
    scaled = (w * np.exp2(127.0 - byte)[:, None, :]).reshape(k, n).astype(np.float32)
    by_word = np.ascontiguousarray(scaled.reshape(k // 512, 128, 4, n).transpose(0, 1, 3, 2))
    if fmt == "e4m3":
        words = by_word.astype(ml_dtypes.float8_e4m3fn).view(np.uint8)
    else:
        c = by_word.astype(ml_dtypes.float4_e2m1fn).view(np.uint8) & 0xF
        words = (c[..., 0::2] | (c[..., 1::2] << 4)).reshape(k // 512, 128, 2 * n)
    return np.ascontiguousarray(words), np.ascontiguousarray(byte.astype(np.uint8).reshape(k // 512, 16, n))


def unpack_weight(words, scales, fmt):
    g, _, n = scales.shape
    words = np.ascontiguousarray(words).reshape(g, 128, n, -1)
    if fmt == "e4m3":
        vals = words.view(ml_dtypes.float8_e4m3fn).astype(np.float64)
    else:
        nib = np.empty((g, 128, n, 4), np.uint8)
        nib[..., 0::2] = words & 0xF
        nib[..., 1::2] = words >> 4
        vals = E2M1[nib]
    vals = vals * np.repeat(np.exp2(scales.astype(np.float64) - 127.0), 8, axis=1)[..., None]
    return vals.transpose(0, 1, 3, 2).reshape(g * 512, n)


D, T, I, Q, J, M = 512, 2048, 512, 128, 512, 2048


def setup_inputs():
    n = np.random.standard_normal
    idx = np.random.permutation(T)[:I]
    idx2 = np.random.permutation(T)[:J]
    idx3 = np.random.permutation(M)[:I]
    fd = mx_kscale(D)
    fj = mx_kscale(J)
    keysp = pack_weight(n((D, T)) / fd[:, None], "e2m1")
    return {
        "query": (n((D, Q)) * 0.6 / np.sqrt(D) * fd[:, None]).astype(np.float32),
        "keys_words": keysp[0],
        "keys_scales": keysp[1],
        "hf": (np.random.uniform(0.5, 2.0, (J, 1)) * fj[:, None]).astype(np.float32),
        "mixer": (n((J, I)) * 0.05 / fj[:, None]).astype(np.float32),
        "pull": (np.random.uniform(0.3, 0.9, (Q, 1))).astype(np.float32),
        "old": (np.random.uniform(0.0, 2.0, (Q, M))).astype(np.float32),
        "fade": (np.random.uniform(0.3, 0.9, (Q, 1))).astype(np.float32),
        "offs": striped(idx),
        "offs2": striped(idx2),
        "offs3": striped(idx3),
    }


def reference(query, keys_words, keys_scales, hf, mixer, pull, old, fade, offs, offs2, offs3):
    idx = unstriped(offs)
    idx2 = unstriped(offs2)
    idx3 = unstriped(offs3)
    keysu = unpack_weight(keys_words, keys_scales, "e2m1")
    keysidx2g = keysu[:, idx2]
    queryq = mxq(f64(query), 0, "e4m3")
    a0 = keysidx2g.T @ queryq
    af = a0 * f64(hf)
    afq = mxq(af, 0, "e4m3")
    mixerq = mxq(f64(mixer), 0, "e4m3")
    mx0 = afq.T @ mixerq
    keysidxg = keysu[:, idx]
    a = queryq.T @ keysidxg
    s = a + mx0
    p = np.exp(s - np.max(s, axis=1, keepdims=True))
    r = p / np.sum(p, axis=1, keepdims=True)
    r1 = np.pad(r, ((0, 0), (1, 0)))[:, :I]
    w = r - r1 * f64(pull)
    ws = w * 256.0
    wf = np.zeros((Q, M))
    wf[:, idx3] = ws
    y = f64(old) * f64(fade) + wf
    return y

@@ -1,0 +1,196 @@
+from contextlib import ExitStack
+
+import concourse.mybir as mybir
+from concourse.masks import make_identity
+
+D, T, I, Q, J, M = 512, 2048, 512, 128, 512, 2048
+FLOPS = 2 * Q * (D * J + J * I + D * I)
+
+F32 = mybir.dt.float32
+BF16 = mybir.dt.bfloat16
+I32 = mybir.dt.int32
+U32 = mybir.dt.uint32
+U16 = mybir.dt.uint16
+U8 = mybir.dt.uint8
+FP8X4 = mybir.dt.float8_e4m3fn_x4
+FP4X4 = mybir.dt.float4_e2m1fn_x4
+ALU = mybir.AluOpType
+ACT = mybir.ActivationFunctionType
+AXIS = mybir.AxisListType
+
+P = 128
+PACK = 4
+MIX_COLS = 256
+OUT_COLS = 512
+FIRST_SLOTS = 128
+LEAD = 16
+
+
+def tile_attend_mixedslots_stepwise_counts_kernel(
+    tc, query, keys_words, keys_scales, hf, mixer, pull, old, fade, offs, offs2, offs3, out
+):
+    nc = tc.nc
+    with ExitStack() as ctx:
+        sb = ctx.enter_context(tc.tile_pool(name="sb", bufs=1))
+        psum = ctx.enter_context(tc.psum_pool(name="psum", bufs=1))
+
+        pool_scales = sb.tile([P, T], U8, name="pool_scales", align_bytes=64)
+        nc.gpsimd.memset(pool_scales[:].bitcast(I32), 0)
+        shares = sb.tile([P, LEAD + I], F32, name="shares")
+        nc.gpsimd.memset(shares[:, 0:LEAD], 0.0)
+        ident = sb.tile([P, P], F32, name="ident")
+        make_identity(nc, ident[:])
+
+        warm = sb.tile([P, 1], F32, name="warm")
+        nc.scalar.activation(warm[:], shares[:, 0:1], ACT.Exp)
+        offs2_sb = sb.tile([P, J // 16], U16, name="offs2_sb")
+        nc.sync.dma_start(offs2_sb[:], offs2)
+        for quad in range(4):
+            nc.sync.dma_start(
+                pool_scales[32 * quad : 32 * quad + 4, :].bitcast(I32),
+                keys_scales[0, 4 * quad : 4 * quad + 4, :].bitcast(I32),
+            )
+        pool_words = sb.tile([P, T], U16, name="pool_words", align_bytes=64)
+        nc.sync.dma_start(pool_words[:].bitcast(I32), keys_words[0].bitcast(I32))
+        query_raw = sb.tile([P, PACK, Q], F32, name="query_raw")
+        nc.sync.dma_start(query_raw[:], query.rearrange("(p t) q -> p t q", t=PACK))
+        mixer_rows = mixer.rearrange("(p t) i -> p t i", t=PACK)
+        mixer_raw = [
+            sb.tile([P, PACK, MIX_COLS], F32, name=f"mixer_raw{c}", tag=f"mixer_raw{c}", align_bytes=64)
+            for c in range(I // MIX_COLS)
+        ]
+        nc.sync.dma_start(mixer_raw[0][:], mixer_rows[:, :, :MIX_COLS])
+        offs_sb = sb.tile([P, I // 16], U16, name="offs_sb")
+        nc.sync.dma_start(offs_sb[:], offs)
+        nc.sync.dma_start(mixer_raw[1][:], mixer_rows[:, :, MIX_COLS:])
+        hf_cols = sb.tile([P, PACK], F32, name="hf_cols")
+        nc.sync.dma_start(hf_cols[:], hf.rearrange("(p t) o -> p (t o)", t=PACK))
+        offs3_sb = sb.tile([P, I // 16], U16, name="offs3_sb")
+        nc.sync.dma_start(offs3_sb[:], offs3)
+        pull_sb = sb.tile([P, 1], F32, name="pull_sb")
+        nc.sync.dma_start(pull_sb[:], pull)
+        fade_sb = sb.tile([P, 1], F32, name="fade_sb")
+        nc.sync.dma_start(fade_sb[:], fade)
+        neg_pull = sb.tile([P, 1], F32, name="neg_pull")
+        nc.gpsimd.tensor_scalar(neg_pull[:], pull_sb[:], -1.0, 0.0, ALU.mult, ALU.add)
+        old_sb = sb.tile([P, M], F32, name="old_sb")
+        nc.sync.dma_start(old_sb[:], old)
+
+        placed = sb.tile([P, M], F32, name="placed")
+        nc.vector.memset(placed[:], 0.0)
+
+        scales2 = sb.tile([P, J], U8, name="scales2", align_bytes=64)
+        nc.vector.tensor_copy(scales2[:], pool_scales[:].indirect(offs2_sb[:]))
+        words2 = sb.tile([P, J], U16, name="words2", align_bytes=64)
+        nc.vector.tensor_copy(words2[:], pool_words[:].indirect(offs2_sb[:]))
+        query_bf = sb.tile([P, Q, PACK], BF16, name="query_bf", align_bytes=64)
+        nc.scalar.copy(query_bf[:], query_raw[:].rearrange("p t q -> p q t"))
+        query_codes = sb.tile([P, Q], U32, name="query_codes", align_bytes=64)
+        query_scales = sb.tile([P, Q], U8, name="query_scales", align_bytes=64)
+        nc.vector.quantize_mx(
+            out=query_codes[:].bitcast(FP8X4),
+            scales=query_scales[:],
+            in_=query_bf[:].rearrange("p q t -> p (q t)"),
+        )
+        a0 = psum.tile([P, J], F32, name="a0", tag="a0")
+        nc.tensor.matmul_mx(
+            out=a0[:],
+            lhsT=query_codes[:].bitcast(FP8X4),
+            lhsT_scale=query_scales[:],
+            rhs=words2[:].bitcast(FP4X4),
+            rhs_scale=scales2[:],
+            start=True,
+            stop=True,
+        )
+        scales1 = sb.tile([P, I], U8, name="scales1", align_bytes=64)
+        nc.vector.tensor_copy(scales1[:], pool_scales[:].indirect(offs_sb[:]))
+        words1 = sb.tile([P, I], U16, name="words1", align_bytes=64)
+        nc.vector.tensor_copy(words1[:], pool_words[:].indirect(offs_sb[:]))
+
+        mixer_codes = sb.tile([P, I], U32, name="mixer_codes", align_bytes=64)
+        mixer_scales = sb.tile([P, I], U8, name="mixer_scales", align_bytes=64)
+        mixer_bf = [
+            sb.tile([P, MIX_COLS, PACK], BF16, name=f"mixer_bf{c}", align_bytes=64) for c in range(I // MIX_COLS)
+        ]
+
+        def weave_mixer(c):
+            nc.scalar.copy(mixer_bf[c][:], mixer_raw[c][:].rearrange("p t i -> p i t"))
+
+        def quantise_mixer(c):
+            cols = slice(c * MIX_COLS, (c + 1) * MIX_COLS)
+            nc.vector.quantize_mx(
+                out=mixer_codes[:, cols].bitcast(FP8X4),
+                scales=mixer_scales[:, cols],
+                in_=mixer_bf[c][:].rearrange("p i t -> p (i t)"),
+            )
+
+        weave_mixer(0)
+        quantise_mixer(0)
+        a0_rows = sb.tile([P, PACK, P], F32, name="a0_rows", tag="mixer_raw0", align_bytes=64)
+        nc.scalar.copy(a0_rows[:], a0[:].rearrange("q (p t) -> q t p", t=PACK))
+        a0_turned = psum.tile([P, PACK, Q], F32, name="a0_turned")
+        for t in range(PACK):
+            nc.tensor.transpose(a0_turned[:, t, :], a0_rows[:, t, :], ident[:])
+        weave_mixer(1)
+        af_bf = sb.tile([P, Q, PACK], BF16, name="af_bf", align_bytes=64)
+        nc.vector.tensor_tensor(
+            af_bf[:],
+            a0_turned[:].rearrange("p t q -> p q t"),
+            hf_cols[:].unsqueeze(1).to_broadcast([P, Q, PACK]),
+            ALU.mult,
+        )
+        quantise_mixer(1)
+        af_codes = sb.tile([P, Q], U32, name="af_codes", align_bytes=64)
+        af_scales = sb.tile([P, Q], U8, name="af_scales", align_bytes=64)
+        nc.vector.quantize_mx(out=af_codes[:].bitcast(FP8X4), scales=af_scales[:], in_=af_bf[:].rearrange("p q t -> p (q t)"))
+
+        scores = psum.tile([P, I], F32, name="scores", tag="a0")
+        nc.tensor.matmul_mx(
+            out=scores[:],
+            lhsT=query_codes[:].bitcast(FP8X4),
+            lhsT_scale=query_scales[:],
+            rhs=words1[:].bitcast(FP4X4),
+            rhs_scale=scales1[:],
+            start=True,
+            stop=False,
+        )
+        nc.tensor.matmul_mx(
+            out=scores[:],
+            lhsT=af_codes[:].bitcast(FP8X4),
+            lhsT_scale=af_scales[:],
+            rhs=mixer_codes[:].bitcast(FP8X4),
+            rhs_scale=mixer_scales[:],
+            start=False,
+            stop=True,
+        )
+
+        neg_max = sb.tile([P, 1], F32, name="neg_max", tag="late")
+        nc.vector.tensor_reduce(neg_max[:], scores[:], AXIS.X, ALU.max, negate=True)
+        pieces = [(0, FIRST_SLOTS), (FIRST_SLOTS, I)]
+        part_sums = [sb.tile([P, 1], F32, name=f"part_sum{n}") for n in range(2)]
+        pulled = [sb.tile([P, hi - lo], F32, name=f"pulled{n}") for n, (lo, hi) in enumerate(pieces)]
+        for n, (lo, hi) in enumerate(pieces):
+            nc.scalar.activation(
+                shares[:, LEAD + lo : LEAD + hi], scores[:, lo:hi], ACT.Exp, bias=neg_max[:], accum_out=part_sums[n][:]
+            )
+            nc.scalar.activation(pulled[n][:], shares[:, LEAD + lo - 1 : LEAD + hi - 1], ACT.Copy, scale=neg_pull[:])
+        row_sum = sb.tile([P, 1], F32, name="row_sum")
+        gain = sb.tile([P, 1], F32, name="gain")
+        for n, (lo, hi) in enumerate(pieces):
+            nc.vector.tensor_tensor(
+                placed[:].indirect(offs3_sb[:, lo // 16 : hi // 16]),
+                shares[:, LEAD + lo : LEAD + hi],
+                pulled[n][:],
+                ALU.add,
+            )
+            if n == 0:
+                nc.vector.tensor_scalar(row_sum[:], part_sums[0][:], part_sums[1][:], 1.0 / 256.0, ALU.add, ALU.mult)
+                nc.vector.reciprocal(gain[:], row_sum[:])
+
+        faded = sb.tile([P, M], F32, name="faded", tag="late")
+        for c in range(M // OUT_COLS):
+            cols = slice(c * OUT_COLS, (c + 1) * OUT_COLS)
+            nc.scalar.activation(faded[:, cols], old_sb[:, cols], ACT.Copy, scale=fade_sb[:])
+            result = sb.tile([P, OUT_COLS], F32, name=f"result{c}")
+            nc.vector.scalar_tensor_tensor(result[:], placed[:, cols], gain[:], faded[:, cols], ALU.mult, ALU.add)
+            nc.sync.dma_start(out[:, cols], result[:])

@@ -34,6 +34,11 @@ def tile_attend_mixedslots_stepwise_counts_kernel(
         sb = ctx.enter_context(tc.tile_pool(name="sb", bufs=1))
         psum = ctx.enter_context(tc.psum_pool(name="psum", bufs=1))
 
+        def weave(woven, planes):
+            nc.scalar.copy(
+                woven[:].rearrange("p (c i) t -> p c t i", i=4), planes[:].rearrange("p t (c i) -> p c t i", i=4)
+            )
+
         pool_scales = sb.tile([P, T], U8, name="pool_scales", align_bytes=64)
         nc.gpsimd.memset(pool_scales[:].bitcast(I32), 0)
         shares = sb.tile([P, LEAD + I], F32, name="shares")
@@ -43,6 +48,8 @@ def tile_attend_mixedslots_stepwise_counts_kernel(
 
         warm = sb.tile([P, 1], F32, name="warm")
         nc.scalar.activation(warm[:], shares[:, 0:1], ACT.Exp)
+        pool_words = sb.tile([P, T], U16, name="pool_words", align_bytes=64)
+        nc.sync.dma_start(pool_words[:].bitcast(I32), keys_words[0].bitcast(I32))
         offs2_sb = sb.tile([P, J // 16], U16, name="offs2_sb")
         nc.sync.dma_start(offs2_sb[:], offs2)
         for quad in range(4):
@@ -50,8 +57,6 @@ def tile_attend_mixedslots_stepwise_counts_kernel(
                 pool_scales[32 * quad : 32 * quad + 4, :].bitcast(I32),
                 keys_scales[0, 4 * quad : 4 * quad + 4, :].bitcast(I32),
             )
-        pool_words = sb.tile([P, T], U16, name="pool_words", align_bytes=64)
-        nc.sync.dma_start(pool_words[:].bitcast(I32), keys_words[0].bitcast(I32))
         query_raw = sb.tile([P, PACK, Q], F32, name="query_raw")
         nc.sync.dma_start(query_raw[:], query.rearrange("(p t) q -> p t q", t=PACK))
         mixer_rows = mixer.rearrange("(p t) i -> p t i", t=PACK)
@@ -79,12 +84,12 @@ def tile_attend_mixedslots_stepwise_counts_kernel(
         placed = sb.tile([P, M], F32, name="placed")
         nc.vector.memset(placed[:], 0.0)
 
-        scales2 = sb.tile([P, J], U8, name="scales2", align_bytes=64)
-        nc.vector.tensor_copy(scales2[:], pool_scales[:].indirect(offs2_sb[:]))
         words2 = sb.tile([P, J], U16, name="words2", align_bytes=64)
         nc.vector.tensor_copy(words2[:], pool_words[:].indirect(offs2_sb[:]))
+        scales2 = sb.tile([P, J], U8, name="scales2", align_bytes=64)
+        nc.vector.tensor_copy(scales2[:], pool_scales[:].indirect(offs2_sb[:]))
         query_bf = sb.tile([P, Q, PACK], BF16, name="query_bf", align_bytes=64)
-        nc.scalar.copy(query_bf[:], query_raw[:].rearrange("p t q -> p q t"))
+        weave(query_bf, query_raw)
         query_codes = sb.tile([P, Q], U32, name="query_codes", align_bytes=64)
         query_scales = sb.tile([P, Q], U8, name="query_scales", align_bytes=64)
         nc.vector.quantize_mx(
@@ -114,7 +119,7 @@ def tile_attend_mixedslots_stepwise_counts_kernel(
         ]
 
         def weave_mixer(c):
-            nc.scalar.copy(mixer_bf[c][:], mixer_raw[c][:].rearrange("p t i -> p i t"))
+            weave(mixer_bf[c], mixer_raw[c])
 
         def quantise_mixer(c):
             cols = slice(c * MIX_COLS, (c + 1) * MIX_COLS)
@@ -174,8 +179,10 @@ def tile_attend_mixedslots_stepwise_counts_kernel(
                 shares[:, LEAD + lo : LEAD + hi], scores[:, lo:hi], ACT.Exp, bias=neg_max[:], accum_out=part_sums[n][:]
             )
             nc.scalar.activation(pulled[n][:], shares[:, LEAD + lo - 1 : LEAD + hi - 1], ACT.Copy, scale=neg_pull[:])
+        both_sums = sb.tile([P, 1], F32, name="both_sums")
+        nc.scalar.activation(both_sums[:], part_sums[0][:], ACT.Identity, bias=part_sums[1][:])
         row_sum = sb.tile([P, 1], F32, name="row_sum")
-        gain = sb.tile([P, 1], F32, name="gain")
+        nc.scalar.activation(row_sum[:], both_sums[:], ACT.Copy, scale=1.0 / 256.0)
         for n, (lo, hi) in enumerate(pieces):
             nc.vector.tensor_tensor(
                 placed[:].indirect(offs3_sb[:, lo // 16 : hi // 16]),
@@ -183,14 +190,17 @@ def tile_attend_mixedslots_stepwise_counts_kernel(
                 pulled[n][:],
                 ALU.add,
             )
-            if n == 0:
-                nc.vector.tensor_scalar(row_sum[:], part_sums[0][:], part_sums[1][:], 1.0 / 256.0, ALU.add, ALU.mult)
-                nc.vector.reciprocal(gain[:], row_sum[:])
+        gain = sb.tile([P, 1], F32, name="gain")
+        nc.vector.reciprocal(gain[:], row_sum[:])
 
         faded = sb.tile([P, M], F32, name="faded", tag="late")
+        result = sb.tile([P, M], F32, name="result")
         for c in range(M // OUT_COLS):
             cols = slice(c * OUT_COLS, (c + 1) * OUT_COLS)
             nc.scalar.activation(faded[:, cols], old_sb[:, cols], ACT.Copy, scale=fade_sb[:])
-            result = sb.tile([P, OUT_COLS], F32, name=f"result{c}")
-            nc.vector.scalar_tensor_tensor(result[:], placed[:, cols], gain[:], faded[:, cols], ALU.mult, ALU.add)
-            nc.sync.dma_start(out[:, cols], result[:])
+        edges = list(range(0, M + 1, 256))
+        for c in range(len(edges) - 1):
+            cols = slice(edges[c], edges[c + 1])
+            nc.vector.scalar_tensor_tensor(result[:, cols], placed[:, cols], gain[:], faded[:, cols], ALU.mult, ALU.add)
+            queue = nc.sync if c % 2 == 0 else nc.scalar
+            queue.dma_start(out[:, cols], result[:, cols])

from contextlib import ExitStack

import concourse.mybir as mybir
from concourse.masks import make_identity

D, T, I, Q, J, M = 512, 2048, 512, 128, 512, 2048
FLOPS = 2 * Q * (D * J + J * I + D * I)

F32 = mybir.dt.float32
BF16 = mybir.dt.bfloat16
I32 = mybir.dt.int32
U32 = mybir.dt.uint32
U16 = mybir.dt.uint16
U8 = mybir.dt.uint8
FP8X4 = mybir.dt.float8_e4m3fn_x4
FP4X4 = mybir.dt.float4_e2m1fn_x4
ALU = mybir.AluOpType
ACT = mybir.ActivationFunctionType
AXIS = mybir.AxisListType

P = 128
PACK = 4
MIX_COLS = 256
OUT_COLS = 512
FIRST_SLOTS = 128
LEAD = 16


def tile_attend_mixedslots_stepwise_counts_kernel(
    tc, query, keys_words, keys_scales, hf, mixer, pull, old, fade, offs, offs2, offs3, out
):
    nc = tc.nc
    with ExitStack() as ctx:
        sb = ctx.enter_context(tc.tile_pool(name="sb", bufs=1))
        psum = ctx.enter_context(tc.psum_pool(name="psum", bufs=1))

        def weave(woven, planes):
            nc.scalar.copy(
                woven[:].rearrange("p (c i) t -> p c t i", i=4), planes[:].rearrange("p t (c i) -> p c t i", i=4)
            )

        pool_scales = sb.tile([P, T], U8, name="pool_scales", align_bytes=64)
        nc.gpsimd.memset(pool_scales[:].bitcast(I32), 0)
        shares = sb.tile([P, LEAD + I], F32, name="shares")
        nc.gpsimd.memset(shares[:, 0:LEAD], 0.0)
        ident = sb.tile([P, P], F32, name="ident")
        make_identity(nc, ident[:])

        warm = sb.tile([P, 1], F32, name="warm")
        nc.scalar.activation(warm[:], shares[:, 0:1], ACT.Exp)
        pool_words = sb.tile([P, T], U16, name="pool_words", align_bytes=64)
        nc.sync.dma_start(pool_words[:].bitcast(I32), keys_words[0].bitcast(I32))
        offs2_sb = sb.tile([P, J // 16], U16, name="offs2_sb")
        nc.sync.dma_start(offs2_sb[:], offs2)
        for quad in range(4):
            nc.sync.dma_start(
                pool_scales[32 * quad : 32 * quad + 4, :].bitcast(I32),
                keys_scales[0, 4 * quad : 4 * quad + 4, :].bitcast(I32),
            )
        query_raw = sb.tile([P, PACK, Q], F32, name="query_raw")
        nc.sync.dma_start(query_raw[:], query.rearrange("(p t) q -> p t q", t=PACK))
        mixer_rows = mixer.rearrange("(p t) i -> p t i", t=PACK)
        mixer_raw = [
            sb.tile([P, PACK, MIX_COLS], F32, name=f"mixer_raw{c}", tag=f"mixer_raw{c}", align_bytes=64)
            for c in range(I // MIX_COLS)
        ]
        nc.sync.dma_start(mixer_raw[0][:], mixer_rows[:, :, :MIX_COLS])
        offs_sb = sb.tile([P, I // 16], U16, name="offs_sb")
        nc.sync.dma_start(offs_sb[:], offs)
        nc.sync.dma_start(mixer_raw[1][:], mixer_rows[:, :, MIX_COLS:])
        hf_cols = sb.tile([P, PACK], F32, name="hf_cols")
        nc.sync.dma_start(hf_cols[:], hf.rearrange("(p t) o -> p (t o)", t=PACK))
        offs3_sb = sb.tile([P, I // 16], U16, name="offs3_sb")
        nc.sync.dma_start(offs3_sb[:], offs3)
        pull_sb = sb.tile([P, 1], F32, name="pull_sb")
        nc.sync.dma_start(pull_sb[:], pull)
        fade_sb = sb.tile([P, 1], F32, name="fade_sb")
        nc.sync.dma_start(fade_sb[:], fade)
        neg_pull = sb.tile([P, 1], F32, name="neg_pull")
        nc.gpsimd.tensor_scalar(neg_pull[:], pull_sb[:], -1.0, 0.0, ALU.mult, ALU.add)
        old_sb = sb.tile([P, M], F32, name="old_sb")
        nc.sync.dma_start(old_sb[:], old)

        placed = sb.tile([P, M], F32, name="placed")
        nc.vector.memset(placed[:], 0.0)

        words2 = sb.tile([P, J], U16, name="words2", align_bytes=64)
        nc.vector.tensor_copy(words2[:], pool_words[:].indirect(offs2_sb[:]))
        scales2 = sb.tile([P, J], U8, name="scales2", align_bytes=64)
        nc.vector.tensor_copy(scales2[:], pool_scales[:].indirect(offs2_sb[:]))
        query_bf = sb.tile([P, Q, PACK], BF16, name="query_bf", align_bytes=64)
        weave(query_bf, query_raw)
        query_codes = sb.tile([P, Q], U32, name="query_codes", align_bytes=64)
        query_scales = sb.tile([P, Q], U8, name="query_scales", align_bytes=64)
        nc.vector.quantize_mx(
            out=query_codes[:].bitcast(FP8X4),
            scales=query_scales[:],
            in_=query_bf[:].rearrange("p q t -> p (q t)"),
        )
        a0 = psum.tile([P, J], F32, name="a0", tag="a0")
        nc.tensor.matmul_mx(
            out=a0[:],
            lhsT=query_codes[:].bitcast(FP8X4),
            lhsT_scale=query_scales[:],
            rhs=words2[:].bitcast(FP4X4),
            rhs_scale=scales2[:],
            start=True,
            stop=True,
        )
        scales1 = sb.tile([P, I], U8, name="scales1", align_bytes=64)
        nc.vector.tensor_copy(scales1[:], pool_scales[:].indirect(offs_sb[:]))
        words1 = sb.tile([P, I], U16, name="words1", align_bytes=64)
        nc.vector.tensor_copy(words1[:], pool_words[:].indirect(offs_sb[:]))

        mixer_codes = sb.tile([P, I], U32, name="mixer_codes", align_bytes=64)
        mixer_scales = sb.tile([P, I], U8, name="mixer_scales", align_bytes=64)
        mixer_bf = [
            sb.tile([P, MIX_COLS, PACK], BF16, name=f"mixer_bf{c}", align_bytes=64) for c in range(I // MIX_COLS)
        ]

        def weave_mixer(c):
            weave(mixer_bf[c], mixer_raw[c])

        def quantise_mixer(c):
            cols = slice(c * MIX_COLS, (c + 1) * MIX_COLS)
            nc.vector.quantize_mx(
                out=mixer_codes[:, cols].bitcast(FP8X4),
                scales=mixer_scales[:, cols],
                in_=mixer_bf[c][:].rearrange("p i t -> p (i t)"),
            )

        weave_mixer(0)
        quantise_mixer(0)
        a0_rows = sb.tile([P, PACK, P], F32, name="a0_rows", tag="mixer_raw0", align_bytes=64)
        nc.scalar.copy(a0_rows[:], a0[:].rearrange("q (p t) -> q t p", t=PACK))
        a0_turned = psum.tile([P, PACK, Q], F32, name="a0_turned")
        for t in range(PACK):
            nc.tensor.transpose(a0_turned[:, t, :], a0_rows[:, t, :], ident[:])
        weave_mixer(1)
        af_bf = sb.tile([P, Q, PACK], BF16, name="af_bf", align_bytes=64)
        nc.vector.tensor_tensor(
            af_bf[:],
            a0_turned[:].rearrange("p t q -> p q t"),
            hf_cols[:].unsqueeze(1).to_broadcast([P, Q, PACK]),
            ALU.mult,
        )
        quantise_mixer(1)
        af_codes = sb.tile([P, Q], U32, name="af_codes", align_bytes=64)
        af_scales = sb.tile([P, Q], U8, name="af_scales", align_bytes=64)
        nc.vector.quantize_mx(out=af_codes[:].bitcast(FP8X4), scales=af_scales[:], in_=af_bf[:].rearrange("p q t -> p (q t)"))

        scores = psum.tile([P, I], F32, name="scores", tag="a0")
        nc.tensor.matmul_mx(
            out=scores[:],
            lhsT=query_codes[:].bitcast(FP8X4),
            lhsT_scale=query_scales[:],
            rhs=words1[:].bitcast(FP4X4),
            rhs_scale=scales1[:],
            start=True,
            stop=False,
        )
        nc.tensor.matmul_mx(
            out=scores[:],
            lhsT=af_codes[:].bitcast(FP8X4),
            lhsT_scale=af_scales[:],
            rhs=mixer_codes[:].bitcast(FP8X4),
            rhs_scale=mixer_scales[:],
            start=False,
            stop=True,
        )

        neg_max = sb.tile([P, 1], F32, name="neg_max", tag="late")
        nc.vector.tensor_reduce(neg_max[:], scores[:], AXIS.X, ALU.max, negate=True)
        pieces = [(0, FIRST_SLOTS), (FIRST_SLOTS, I)]
        part_sums = [sb.tile([P, 1], F32, name=f"part_sum{n}") for n in range(2)]
        pulled = [sb.tile([P, hi - lo], F32, name=f"pulled{n}") for n, (lo, hi) in enumerate(pieces)]
        for n, (lo, hi) in enumerate(pieces):
            nc.scalar.activation(
                shares[:, LEAD + lo : LEAD + hi], scores[:, lo:hi], ACT.Exp, bias=neg_max[:], accum_out=part_sums[n][:]
            )
            nc.scalar.activation(pulled[n][:], shares[:, LEAD + lo - 1 : LEAD + hi - 1], ACT.Copy, scale=neg_pull[:])
        both_sums = sb.tile([P, 1], F32, name="both_sums")
        nc.scalar.activation(both_sums[:], part_sums[0][:], ACT.Identity, bias=part_sums[1][:])
        row_sum = sb.tile([P, 1], F32, name="row_sum")
        nc.scalar.activation(row_sum[:], both_sums[:], ACT.Copy, scale=1.0 / 256.0)
        for n, (lo, hi) in enumerate(pieces):
            nc.vector.tensor_tensor(
                placed[:].indirect(offs3_sb[:, lo // 16 : hi // 16]),
                shares[:, LEAD + lo : LEAD + hi],
                pulled[n][:],
                ALU.add,
            )
        gain = sb.tile([P, 1], F32, name="gain")
        nc.vector.reciprocal(gain[:], row_sum[:])

        faded = sb.tile([P, M], F32, name="faded", tag="late")
        result = sb.tile([P, M], F32, name="result")
        for c in range(M // OUT_COLS):
            cols = slice(c * OUT_COLS, (c + 1) * OUT_COLS)
            nc.scalar.activation(faded[:, cols], old_sb[:, cols], ACT.Copy, scale=fade_sb[:])
        edges = list(range(0, M + 1, 256))
        for c in range(len(edges) - 1):
            cols = slice(edges[c], edges[c + 1])
            nc.vector.scalar_tensor_tensor(result[:, cols], placed[:, cols], gain[:], faded[:, cols], ALU.mult, ALU.add)
            queue = nc.sync if c % 2 == 0 else nc.scalar
            queue.dma_start(out[:, cols], result[:, cols])
